import numpy as np
import ml_dtypes

BF16 = ml_dtypes.bfloat16


def bf(x):
    return np.asarray(x, np.float32).astype(BF16)


def f32(x):
    return np.asarray(x, np.float32)


def f64(x):
    return np.asarray(x).astype(np.float64)


def striped(idx):
    return np.tile(idx.reshape(-1, 16).T, (8, 1))


S, K, M, N, B, Q = 512, 256, 256, 384, 2, 192


def setup_inputs():
    return {"base": bf(np.random.standard_normal((B, M, S))), "x": bf(np.random.standard_normal((K, N))), "w": bf(np.random.standard_normal((K, M)) / np.sqrt(K)), "b": f32(0.5 * np.random.standard_normal((M, 1))), "offs": striped(np.random.permutation(S)[:N])}


def reference(base, x, w, b, offs):
    idx = offs[:16].T.reshape(-1)
    z = f64(base).copy()
    for i in range(B):
        z[i][:, idx[i * Q : (i + 1) * Q]] += f64(w).T @ f64(x)[:, i * Q : (i + 1) * Q]
    return z + f64(b)

@@ -1,0 +1,56 @@
+import concourse.mybir as mybir
+from concourse.masks import make_identity
+
+BF16, F32, U16 = mybir.dt.bfloat16, mybir.dt.float32, mybir.dt.uint16
+P = 128
+
+B, M, S = 2, 256, 512
+K, N = 256, 384
+Q = N // B
+A = M // P
+C = K // P
+
+FLOPS = 2 * M * K * N
+
+
+def tile_scatter_matmul_kernel(tc, base, x, w, b, offs, out):
+    nc = tc.nc
+    with (
+        tc.tile_pool(name="held", bufs=1) as held,
+        tc.psum_pool(name="windows", bufs=1) as windows,
+    ):
+        base_sb = [held.tile([P, A * S], BF16, name=f"base{i}") for i in range(B)]
+        offs_sb = held.tile([P, N // 16], U16, name="offs_sb")
+        w_sb = held.tile([P, C * M], BF16, name="w_sb")
+        x_sb = held.tile([P, C * N], BF16, name="x_sb")
+        bias_sb = held.tile([P, A], F32, name="bias_sb")
+        for i in range(B):
+            nc.sync.dma_start(base_sb[i][:], base[i].rearrange("(p a) t -> p (a t)", a=A))
+        nc.sync.dma_start(offs_sb[:], offs)
+        nc.sync.dma_start(w_sb[:], w.rearrange("(p c) m -> p (c m)", c=C))
+        nc.sync.dma_start(x_sb[:], x.rearrange("(p c) n -> p (c n)", c=C))
+        nc.sync.dma_start(bias_sb[:], b.rearrange("(p a) o -> p (a o)", a=A))
+
+        ident = held.tile([P, P], BF16, name="ident")
+        make_identity(nc, ident[:])
+
+        pairs = [(i, a) for i in range(B) for a in range(A)]
+        window = {(i, a): windows.tile([P, S], F32, name=f"window{i}_{a}") for i, a in pairs}
+        for i, a in pairs:
+            nc.tensor.matmul(window[i, a][:], ident[:], base_sb[i][:, a * S : (a + 1) * S], start=True, stop=False)
+
+        for i, a in pairs:
+            piece = offs_sb[:, i * (Q // 16) : (i + 1) * (Q // 16)]
+            for c in range(C):
+                weights = w_sb[:, c * M + a : (c + 1) * M : A]
+                moving = x_sb[:, c * N + i * Q : c * N + (i + 1) * Q]
+                nc.tensor.matmul(window[i, a][:].indirect(piece), weights, moving, start=False, stop=(c == C - 1))
+
+        for i, a in pairs:
+            z = held.tile([P, S], F32, name=f"z{i}_{a}")
+            bias = bias_sb[:, a : a + 1]
+            if a == 0:
+                nc.vector.tensor_scalar(z[:], window[i, a][:], bias, None, mybir.AluOpType.add)
+            else:
+                nc.scalar.activation(z[:], window[i, a][:], mybir.ActivationFunctionType.Identity, bias=bias)
+            nc.sync.dma_start(out[i].rearrange("(p a) t -> p a t", a=A)[:, a, :], z[:])

@@ -10,6 +10,8 @@ Q = N // B
 A = M // P
 C = K // P
 
+WARM_UPS = 5
+
 FLOPS = 2 * M * K * N
 
 
@@ -30,6 +32,12 @@ def tile_scatter_matmul_kernel(tc, base, x, w, b, offs, out):
         nc.sync.dma_start(w_sb[:], w.rearrange("(p c) m -> p (c m)", c=C))
         nc.sync.dma_start(x_sb[:], x.rearrange("(p c) n -> p (c n)", c=C))
         nc.sync.dma_start(bias_sb[:], b.rearrange("(p a) o -> p (a o)", a=A))
+
+        zeros = held.tile([P, S], BF16, name="zeros")
+        nc.vector.memset(zeros[:], 0.0)
+        spare = windows.tile([P, S], F32, name="spare")
+        for step in range(WARM_UPS):
+            nc.tensor.matmul(spare[:], zeros[:, :P], zeros[:], start=True, stop=True)
 
         ident = held.tile([P, P], BF16, name="ident")
         make_identity(nc, ident[:])

@@ -36,6 +36,8 @@ def tile_scatter_matmul_kernel(tc, base, x, w, b, offs, out):
         zeros = held.tile([P, S], BF16, name="zeros")
         nc.vector.memset(zeros[:], 0.0)
         spare = windows.tile([P, S], F32, name="spare")
+        warm = held.tile([P, 1], F32, name="warm")
+        nc.scalar.activation(warm[:], zeros[:, :1], mybir.ActivationFunctionType.Identity)
         for step in range(WARM_UPS):
             nc.tensor.matmul(spare[:], zeros[:, :P], zeros[:], start=True, stop=True)
 

@@ -10,7 +10,7 @@ Q = N // B
 A = M // P
 C = K // P
 
-WARM_UPS = 5
+WARM_UPS = 3
 
 FLOPS = 2 * M * K * N
 
@@ -56,11 +56,15 @@ def tile_scatter_matmul_kernel(tc, base, x, w, b, offs, out):
                 moving = x_sb[:, c * N + i * Q : c * N + (i + 1) * Q]
                 nc.tensor.matmul(window[i, a][:].indirect(piece), weights, moving, start=False, stop=(c == C - 1))
 
+        H = S // 2
         for i, a in pairs:
-            z = held.tile([P, S], F32, name=f"z{i}_{a}")
+            rows = out[i].rearrange("(p a) t -> p a t", a=A)[:, a, :]
             bias = bias_sb[:, a : a + 1]
-            if a == 0:
-                nc.vector.tensor_scalar(z[:], window[i, a][:], bias, None, mybir.AluOpType.add)
-            else:
-                nc.scalar.activation(z[:], window[i, a][:], mybir.ActivationFunctionType.Identity, bias=bias)
-            nc.sync.dma_start(out[i].rearrange("(p a) t -> p a t", a=A)[:, a, :], z[:])
+            for h in range(2):
+                half = slice(h * H, (h + 1) * H)
+                z = held.tile([P, H], F32, name=f"z{i}_{a}_{h}")
+                if a == 0:
+                    nc.vector.tensor_scalar(z[:], window[i, a][:, half], bias, None, mybir.AluOpType.add)
+                else:
+                    nc.scalar.activation(z[:], window[i, a][:, half], mybir.ActivationFunctionType.Identity, bias=bias)
+                nc.sync.dma_start(rows[:, half], z[:])

import concourse.mybir as mybir
from concourse.masks import make_identity

BF16, F32, U16 = mybir.dt.bfloat16, mybir.dt.float32, mybir.dt.uint16
P = 128

B, M, S = 2, 256, 512
K, N = 256, 384
Q = N // B
A = M // P
C = K // P

WARM_UPS = 3

FLOPS = 2 * M * K * N


def tile_scatter_matmul_kernel(tc, base, x, w, b, offs, out):
    nc = tc.nc
    with (
        tc.tile_pool(name="held", bufs=1) as held,
        tc.psum_pool(name="windows", bufs=1) as windows,
    ):
        base_sb = [held.tile([P, A * S], BF16, name=f"base{i}") for i in range(B)]
        offs_sb = held.tile([P, N // 16], U16, name="offs_sb")
        w_sb = held.tile([P, C * M], BF16, name="w_sb")
        x_sb = held.tile([P, C * N], BF16, name="x_sb")
        bias_sb = held.tile([P, A], F32, name="bias_sb")
        for i in range(B):
            nc.sync.dma_start(base_sb[i][:], base[i].rearrange("(p a) t -> p (a t)", a=A))
        nc.sync.dma_start(offs_sb[:], offs)
        nc.sync.dma_start(w_sb[:], w.rearrange("(p c) m -> p (c m)", c=C))
        nc.sync.dma_start(x_sb[:], x.rearrange("(p c) n -> p (c n)", c=C))
        nc.sync.dma_start(bias_sb[:], b.rearrange("(p a) o -> p (a o)", a=A))

        zeros = held.tile([P, S], BF16, name="zeros")
        nc.vector.memset(zeros[:], 0.0)
        spare = windows.tile([P, S], F32, name="spare")
        warm = held.tile([P, 1], F32, name="warm")
        nc.scalar.activation(warm[:], zeros[:, :1], mybir.ActivationFunctionType.Identity)
        for step in range(WARM_UPS):
            nc.tensor.matmul(spare[:], zeros[:, :P], zeros[:], start=True, stop=True)

        ident = held.tile([P, P], BF16, name="ident")
        make_identity(nc, ident[:])

        pairs = [(i, a) for i in range(B) for a in range(A)]
        window = {(i, a): windows.tile([P, S], F32, name=f"window{i}_{a}") for i, a in pairs}
        for i, a in pairs:
            nc.tensor.matmul(window[i, a][:], ident[:], base_sb[i][:, a * S : (a + 1) * S], start=True, stop=False)

        for i, a in pairs:
            piece = offs_sb[:, i * (Q // 16) : (i + 1) * (Q // 16)]
            for c in range(C):
                weights = w_sb[:, c * M + a : (c + 1) * M : A]
                moving = x_sb[:, c * N + i * Q : c * N + (i + 1) * Q]
                nc.tensor.matmul(window[i, a][:].indirect(piece), weights, moving, start=False, stop=(c == C - 1))

        H = S // 2
        for i, a in pairs:
            rows = out[i].rearrange("(p a) t -> p a t", a=A)[:, a, :]
            bias = bias_sb[:, a : a + 1]
            for h in range(2):
                half = slice(h * H, (h + 1) * H)
                z = held.tile([P, H], F32, name=f"z{i}_{a}_{h}")
                if a == 0:
                    nc.vector.tensor_scalar(z[:], window[i, a][:, half], bias, None, mybir.AluOpType.add)
                else:
                    nc.scalar.activation(z[:], window[i, a][:, half], mybir.ActivationFunctionType.Identity, bias=bias)
                nc.sync.dma_start(rows[:, half], z[:])
